import numpy as np
import ml_dtypes


def mxq(x, axis, fmt="e4m3"):
    dtype, down = {"e4m3": (ml_dtypes.float8_e4m3fn, 7), "e5m2": (ml_dtypes.float8_e5m2, 14)}[fmt]
    v = np.moveaxis(np.asarray(x, np.float32).astype(ml_dtypes.bfloat16).astype(np.float64), axis, -1)
    blocks = v.reshape(v.shape[:-1] + (-1, 32))
    amax = np.abs(blocks).max(-1, keepdims=True)
    byte = np.maximum(np.where(amax > 0, np.frexp(amax)[1] - 1 + 127, 0) - down, 1)
    scale = np.exp2(byte - 127.0)
    codes = (blocks / scale).astype(np.float32).astype(dtype).astype(np.float64)
    return np.moveaxis((codes * scale).reshape(v.shape), -1, axis)


WIDE = False


def mx_kscale(k):
    if not WIDE:
        return np.ones(k)
    levels = np.array([10, -10, 5, -5, 0])
    if k % 512:
        return np.exp2(np.random.permutation(np.resize(levels, k // 32))).repeat(32)
    a = np.empty((k // 512, 16))
    for p in range(k // 512):
        a[p, :8] = np.random.permutation(np.resize(levels, 8))
        for g in range(8):
            far = levels[np.abs(levels - a[p, g]) >= 10]
            a[p, g + 8] = far[np.random.randint(len(far))]
    return np.exp2(a.ravel()).repeat(32)


def f64(x):
    return np.asarray(x).astype(np.float64)


def striped(idx):
    return np.tile(idx.reshape(-1, 16).T, (8, 1)).astype(np.uint16)


def unstriped(offs):
    return offs[:16].T.reshape(-1).astype(np.int64)


E2M1 = np.array([0.0, 0.5, 1.0, 1.5, 2.0, 3.0, 4.0, 6.0, -0.0, -0.5, -1.0, -1.5, -2.0, -3.0, -4.0, -6.0])


def pack_weight(w, fmt):
    k, n = w.shape
    w = f64(np.asarray(w, np.float32).astype(ml_dtypes.bfloat16)).reshape(k // 32, 32, n)
    amax = np.abs(w).max(1)
    if fmt == "e4m3":
        byte = np.frexp(amax)[1] - 1 + 127 - 7
    else:
        mant, ex = np.frexp(amax / 6.0)
        byte = np.where(mant > 0.5, ex, ex - 1) + 127
    byte = np.clip(np.where(amax > 0, byte, 1), 1, 254)
    scaled = (w * np.exp2(127.0 - byte)[:, None, :]).reshape(k, n).astype(np.float32)
    by_word = np.ascontiguousarray(scaled.reshape(k // 512, 128, 4, n).transpose(0, 1, 3, 2))
    if fmt == "e4m3":
        words = by_word.astype(ml_dtypes.float8_e4m3fn).view(np.uint8)
    else:
        c = by_word.astype(ml_dtypes.float4_e2m1fn).view(np.uint8) & 0xF
        words = (c[..., 0::2] | (c[..., 1::2] << 4)).reshape(k // 512, 128, 2 * n)
    return np.ascontiguousarray(words), np.ascontiguousarray(byte.astype(np.uint8).reshape(k // 512, 16, n))


def unpack_weight(words, scales, fmt):
    g, _, n = scales.shape
    words = np.ascontiguousarray(words).reshape(g, 128, n, -1)
    if fmt == "e4m3":
        vals = words.view(ml_dtypes.float8_e4m3fn).astype(np.float64)
    else:
        nib = np.empty((g, 128, n, 4), np.uint8)
        nib[..., 0::2] = words & 0xF
        nib[..., 1::2] = words >> 4
        vals = E2M1[nib]
    vals = vals * np.repeat(np.exp2(scales.astype(np.float64) - 127.0), 8, axis=1)[..., None]
    return vals.transpose(0, 1, 3, 2).reshape(g * 512, n)


def gelu(v):
    return 0.5 * v * (1.0 + np.tanh(np.sqrt(2.0 / np.pi) * (v + 0.044715 * v**3)))


K, M, T, S, P, H, N, T2 = 1024, 512, 2048, 1024, 512, 1024, 512, 2048

def setup_inputs():
    n = np.random.standard_normal
    s, s2, u = mx_kscale(K)[:, None], mx_kscale(M)[:, None], mx_kscale(H)[:, None]
    tab_words, tab_scales = pack_weight(n((K, T)) * s, "e4m3")
    tab2_words, tab2_scales = pack_weight(n((M, T)) * s2, "e4m3")
    w2_words, w2_scales = pack_weight(1.8 * n((M, H)) / np.sqrt(M) / s2, "e2m1")
    w4_words, w4_scales = pack_weight(n((H, N)) / np.sqrt(H) / u, "e2m1")
    w5_words, w5_scales = pack_weight(n((H, N)) / np.sqrt(H) / u, "e4m3")
    perm = np.random.permutation(T2)
    return {
        "tab_words": tab_words, "tab_scales": tab_scales,
        "tab2_words": tab2_words, "tab2_scales": tab2_scales,
        "offs": striped(np.random.permutation(T)[:S]),
        "offs2": striped(np.random.permutation(T)[:P]),
        "pos1": striped(np.random.permutation(S)[:P]),
        "offs3": striped(perm[:S]), "offs4": striped(perm[S:S + P]),
        "w1": (n((K, H)) / np.sqrt(K) / s * u.T).astype(np.float32),
        "w2_words": w2_words, "w2_scales": w2_scales,
        "amp": (np.exp(0.3 * n(H)) * u[:, 0]).astype(np.float32),
        "w3": (n((H, N)) / np.sqrt(H) / u).astype(np.float32),
        "w4_words": w4_words, "w4_scales": w4_scales,
        "w5_words": w5_words, "w5_scales": w5_scales,
        "page1": n((N, T2)).astype(np.float32),
        "wg1": np.exp(0.3 * n((128, S))).astype(np.float32),
        "wg2": np.exp(0.3 * n((128, P))).astype(np.float32)}

def reference(tab_words, tab_scales, tab2_words, tab2_scales, offs, offs2, pos1, offs3, offs4, w1, w2_words, w2_scales, amp, w3, w4_words, w4_scales, w5_words, w5_scales, page1, wg1, wg2):
    v = unpack_weight(tab_words, tab_scales, "e4m3")[:, unstriped(offs)]
    v2 = unpack_weight(tab2_words, tab2_scales, "e4m3")[:, unstriped(offs2)]
    h1 = mxq(f64(w1), 0, "e4m3").T @ v
    h2 = unpack_weight(w2_words, w2_scales, "e2m1").T @ v2
    z1 = mxq(np.abs(h1), 0, "e4m3")
    z2 = mxq(f64(amp)[:, None] * np.tanh(h2) + h1[:, unstriped(pos1)], 0, "e4m3")
    y1 = mxq(f64(w3), 0, "e4m3").T @ z1
    ya = unpack_weight(w4_words, w4_scales, "e2m1").T @ z2
    yb = unpack_weight(w5_words, w5_scales, "e4m3").T @ z2
    y2 = ya * yb
    out = f64(page1).copy()
    out[:, unstriped(offs3)] = np.tile(f64(wg1), (N // 128, 1)) * y1
    out[:, unstriped(offs4)] = np.tile(f64(wg2), (N // 128, 1)) * y2
    return out

@@ -1,0 +1,335 @@
+from contextlib import ExitStack
+
+import concourse.mybir as mybir
+from concourse.masks import make_identity
+
+K, M, T, S, PA, H, N, T2 = 1024, 512, 2048, 1024, 512, 1024, 512, 2048
+FLOPS = 2 * (K * H * S + M * H * PA + H * N * S + 2 * H * N * PA)
+
+F32 = mybir.dt.float32
+BF16 = mybir.dt.bfloat16
+I32 = mybir.dt.int32
+U32 = mybir.dt.uint32
+U16 = mybir.dt.uint16
+U8 = mybir.dt.uint8
+FP8X4 = mybir.dt.float8_e4m3fn_x4
+FP4X4 = mybir.dt.float4_e2m1fn_x4
+ACT = mybir.ActivationFunctionType
+ALU = mybir.AluOpType
+
+P = 128
+
+
+def tile_list_wire_laundering_features_kernel(
+    tc, tab_words, tab_scales, tab2_words, tab2_scales, offs, offs2, pos1, offs3, offs4,
+    w1, w2_words, w2_scales, amp, w3, w4_words, w4_scales, w5_words, w5_scales, page1, wg1, wg2, out,
+):
+    nc = tc.nc
+    with ExitStack() as ctx:
+        held = ctx.enter_context(tc.tile_pool(name="held", bufs=1))
+        ring = ctx.enter_context(tc.tile_pool(name="ring", bufs=1))
+        psum = ctx.enter_context(tc.psum_pool(name="psum", bufs=1))
+
+        def keep(shape, dtype, name):
+            return held.tile(shape, dtype, name=name, align_bytes=64)
+
+        def wide(shape, name):
+            return ring.tile(shape, F32, name=name, tag="wide", bufs=5, align_bytes=64)
+
+        def load_list(src, name):
+            lst = keep([P, src.shape[1]], U16, name)
+            nc.sync.dma_start(lst[:], src)
+            return lst
+
+        def load_words(src, name):
+            words = keep([P, src.shape[1]], I32, name)
+            nc.sync.dma_start(words[:], src.rearrange("p t i -> p (t i)").bitcast(I32))
+            return words
+
+        def zeroed(width, name, engine):
+            plane = keep([P, width], U8, name)
+            engine.memset(plane[:].bitcast(I32), 0)
+            return plane
+
+        def load_scales_side_by_side(plane, src):
+            passes = src.shape[0]
+            for q in range(4):
+                nc.sync.dma_start(
+                    plane[32 * q : 32 * q + 4, :].bitcast(I32).rearrange("r (a c) -> r a c", a=passes),
+                    src[:, 4 * q : 4 * q + 4, :].bitcast(I32).rearrange("a r c -> r a c"),
+                )
+
+        def gather_words(got, words, lst):
+            nc.vector.tensor_copy(got, words[:].bitcast(U32).indirect(lst))
+
+        def gather_scales(got, plane, lst):
+            nc.vector.tensor_copy(got, plane[:].indirect(lst))
+
+        def quantize(codes, scales, grouped):
+            nc.vector.quantize_mx(out=codes.bitcast(FP8X4), scales=scales, in_=grouped)
+
+        tab2_sc = zeroed(T, "tab2_sc", nc.gpsimd)
+        w2_sc = zeroed(H, "w2_sc", nc.gpsimd)
+        tab_sc = zeroed(T, "tab_sc", nc.vector)
+        w4_sc = zeroed(2 * N, "w4_sc", nc.vector)
+        w5_sc = zeroed(2 * N, "w5_sc", nc.vector)
+        ident = keep([P, P], F32, "ident")
+        make_identity(nc, ident[:])
+
+        load_scales_side_by_side(tab2_sc, tab2_scales)
+        idx2 = load_list(offs2, "idx2")
+        tab2_w = load_words(tab2_words[0], "tab2_w")
+        w2_w = keep([P, 2 * H], U8, "w2_w")
+        nc.sync.dma_start(w2_w[:].bitcast(I32), w2_words[0].bitcast(I32))
+        idx = load_list(offs, "idx")
+        load_scales_side_by_side(w2_sc, w2_scales)
+        tab_w = [load_words(tab_words[0], "tab_w0")]
+        w1_raw = {}
+
+        def load_w1(a, b):
+            w1_raw[a, b] = wide([P, 4, 512], "w1_raw")
+            rows = w1[512 * a : 512 * a + 512, 512 * b : 512 * b + 512]
+            nc.sync.dma_start(w1_raw[a, b][:], rows.rearrange("(p i) c -> p i c", i=4))
+
+        w3_raw = {}
+
+        def load_w3(g):
+            w3_raw[g] = wide([P, 2, 4, 256], "w3_raw")
+            for b in range(2):
+                rows = w3[512 * b : 512 * b + 512, 256 * g : 256 * g + 256]
+                nc.sync.dma_start(w3_raw[g][:, b], rows.rearrange("(p i) c -> p i c", i=4))
+
+        page = {}
+
+        def load_page(nt):
+            page[nt] = held.tile([P, T2], F32, name="page", tag="page%d" % nt, align_bytes=64)
+            nc.sync.dma_start(page[nt][:], page1[P * nt : P * nt + P, :])
+
+        wg1_sb = {}
+
+        def load_wg1(h):
+            wg1_sb[h] = keep([P, 512], F32, "wg1_sb%d" % h)
+            nc.sync.dma_start(wg1_sb[h][:], wg1[:, 512 * h : 512 * h + 512])
+
+        load_w1(0, 0)
+        for q in range(4):
+            nc.sync.dma_start(tab_sc[32 * q : 32 * q + 8, :].bitcast(I32), tab_scales[:, 4 * q : 4 * q + 4, :].bitcast(I32))
+        amp_sb = keep([P, 2, 4], F32, "amp_sb")
+        nc.sync.dma_start(amp_sb[:], amp.rearrange("(b p t) -> p b t", b=2, t=4))
+        load_w1(1, 0)
+        load_w1(0, 1)
+        load_w1(1, 1)
+        tab_w.append(load_words(tab_words[1], "tab_w1"))
+        load_w3(0)
+        idx3 = load_list(offs3, "idx3")
+        load_wg1(0)
+        load_page(0)
+        load_page(1)
+        load_w3(1)
+        load_page(2)
+        load_page(3)
+        load_wg1(1)
+        p1 = load_list(pos1, "p1")
+        w4_w = keep([P, 2, 2 * N], U8, "w4_w")
+        nc.sync.dma_start(w4_w[:].bitcast(I32), w4_words.bitcast(I32).rearrange("a p c -> p a c"))
+        load_scales_side_by_side(w4_sc, w4_scales)
+        w5_w = keep([P, 2, N], I32, "w5_w")
+        nc.sync.dma_start(w5_w[:], w5_words.rearrange("a p c i -> p a (c i)").bitcast(I32))
+        load_scales_side_by_side(w5_sc, w5_scales)
+        wg2_sb = keep([P, PA], F32, "wg2_sb")
+        nc.sync.dma_start(wg2_sb[:], wg2)
+        idx4 = load_list(offs4, "idx4")
+
+        w1_c, w1_sc = {}, {}
+        v_w = [keep([P, S], U32, "v_w%d" % a) for a in range(2)]
+        v_sc = keep([P, S], U8, "v_sc")
+
+        def quantize_w1(a, b, split):
+            grouped = ring.tile([P, 4, P, 4], BF16, name="w_grouped", tag="w_grouped", bufs=2, align_bytes=64)
+            dst = grouped[:].rearrange("p t m i -> p m t i")
+            src = w1_raw[a, b][:].rearrange("p i (m t) -> p m t i", t=4)
+            if split:
+                nc.scalar.copy(dst[:, :split], src[:, :split])
+            nc.vector.tensor_copy(dst[:, split:], src[:, split:])
+            w1_c[a, b] = keep([P, 512], U32, "w1_c%d%d" % (a, b))
+            w1_sc[a, b] = keep([P, 512], U8, "w1_sc%d%d" % (a, b))
+            quantize(w1_c[a, b][:], w1_sc[a, b][:], grouped[:].rearrange("p t m i -> p (t m i)"))
+
+        w3_c, w3_sc = {}, {}
+
+        def quantize_w3(g, copy):
+            grouped = ring.tile([P, 2, 256, 4], BF16, name="w_grouped", tag="w_grouped", bufs=2, align_bytes=64)
+            for b in range(2):
+                copy(grouped[:, b].rearrange("p (c e) i -> p c i e", e=4), w3_raw[g][:, b].rearrange("p i (c e) -> p c i e", e=4))
+            w3_c[g] = keep([P, 512], U32, "w3_c%d" % g)
+            w3_sc[g] = keep([P, 512], U8, "w3_sc%d" % g)
+            quantize(w3_c[g][:], w3_sc[g][:], grouped[:].rearrange("p b c i -> p (b c i)"))
+
+        v2_w = keep([P, PA], U32, "v2_w")
+        v2_sc = keep([P, PA], U8, "v2_sc")
+        gather_words(v2_w[:], tab2_w, idx2[:])
+        gather_scales(v2_sc[:], tab2_sc, idx2[:])
+        tanh_t, gated = {}, {}
+        for b in range(2):
+            for u in range(4):
+                tanh_t[b, u] = ring.tile([P, 4, P], F32, name="tanh_t", tag=("y", "z1_grouped")[b], bufs=4, align_bytes=64)
+                bank = psum.tile([P, 512], F32, name="h2_bank", tag="bank0", bufs=3)
+                nc.tensor.matmul_mx(
+                    bank[:],
+                    lhsT=v2_w[:, P * u : P * u + P].bitcast(FP8X4),
+                    lhsT_scale=v2_sc[:, P * u : P * u + P],
+                    rhs=w2_w[:, 1024 * b : 1024 * b + 1024].bitcast(FP4X4),
+                    rhs_scale=w2_sc[:, 512 * b : 512 * b + 512],
+                    start=True,
+                    stop=True,
+                )
+                nc.scalar.activation(tanh_t[b, u][:], bank[:].rearrange("p (m t) -> p t m", t=4), ACT.Tanh)
+        for b in range(2):
+            gated[b] = keep([P, 4, PA], F32, "gated%d" % b)
+            for t in range(4):
+                bank = psum.tile([P, 512], F32, name="turn_bank", tag="bank1", bufs=3)
+                for u in range(4):
+                    nc.tensor.transpose(bank[:, P * u : P * u + P], tanh_t[b, u][:, t, :], ident[:])
+                nc.scalar.activation(gated[b][:, t, :], bank[:], ACT.Copy, scale=amp_sb[:, b, t : t + 1])
+
+        gather_words(v_w[0][:], tab_w[0], idx[:])
+        gather_scales(v_sc[:], tab_sc, idx[:])
+        quantize_w1(0, 0, 0)
+        quantize_w1(1, 0, 0)
+        quantize_w1(0, 1, 0)
+        quantize_w1(1, 1, 96)
+        for j0, n in ((0, 256), (256, 256), (512, 512)):
+            gather_words(v_w[1][:, j0 : j0 + n], tab_w[1], idx[:, j0 // 16 : (j0 + n) // 16])
+        quantize_w3(0, nc.vector.tensor_copy)
+
+        h1 = {(b, t): held.tile([P, S], F32, name="h1", tag="h1_%d%d" % (b, t), align_bytes=64) for b in range(2) for t in range(4)}
+        z1_c = [keep([P, S], U32, "z1_c%d" % b) for b in range(2)]
+        z1_sc = [keep([P, S], U8, "z1_sc%d" % b) for b in range(2)]
+
+        def first_stage(jq):
+            banks = {}
+            for b in range(2):
+                grouped = ring.tile([P, 256, 4], BF16, name="z1_grouped", tag="z1_grouped", bufs=4, align_bytes=64)
+                for u in range(2):
+                    j0 = 256 * jq + P * u
+                    bank = psum.tile([P, 4, P], F32, name="h1_bank", tag="bank%d" % b, bufs=3)
+                    for t in range(4):
+                        for a in (1, 0):
+                            nc.tensor.matmul_mx(
+                                bank[:, t, :],
+                                lhsT=w1_c[a, b][:, P * t : P * t + P].bitcast(FP8X4),
+                                lhsT_scale=w1_sc[a, b][:, P * t : P * t + P],
+                                rhs=v_w[a][:, j0 : j0 + P].bitcast(FP8X4),
+                                rhs_scale=v_sc[4 * a : P, j0 : j0 + P],
+                                start=(a == 1),
+                                stop=(a == 0),
+                            )
+                    nc.scalar.activation(grouped[:, P * u : P * u + P, :], bank[:].rearrange("p t j -> p j t"), ACT.Abs)
+                    banks[b, u] = bank
+                cols = slice(256 * jq, 256 * jq + 256)
+                quantize(z1_c[b][:, cols], z1_sc[b][:, cols], grouped[:].rearrange("p j t -> p (j t)"))
+            return banks
+
+        def keep_h1(jq, banks, which):
+            for b, u in which:
+                j0 = 256 * jq + P * u
+                for t in range(4):
+                    nc.scalar.copy(h1[b, t][:, j0 : j0 + P], banks[b, u][:, t, :])
+
+        def put_y1(nt, j0, n, behind=None):
+            g, c0 = divmod(P * nt, 256)
+            bank = psum.tile([P, 512], F32, name="y_bank", tag="y_bank", bufs=2)
+            for b in range(2):
+                nc.tensor.matmul_mx(
+                    bank[:, 0:n],
+                    lhsT=w3_c[g][:, 256 * b + c0 : 256 * b + c0 + P].bitcast(FP8X4),
+                    lhsT_scale=w3_sc[g][:, 256 * b + c0 : 256 * b + c0 + P],
+                    rhs=z1_c[b][:, j0 : j0 + n].bitcast(FP8X4),
+                    rhs_scale=z1_sc[b][:, j0 : j0 + n],
+                    start=(b == 0),
+                    stop=(b == 1),
+                )
+            if behind is None:
+                y = ring.tile([P, n], F32, name="y", tag="y", bufs=4, align_bytes=64)
+            else:
+                y = held.tile([P, n], F32, name="y", tag=behind, align_bytes=64)
+            nc.scalar.copy(y[:], bank[:, 0:n])
+            h, c1 = divmod(j0, 512)
+            nc.vector.tensor_tensor(page[nt][:].indirect(idx3[:, j0 // 16 : (j0 + n) // 16]), y[:], wg1_sb[h][:, c1 : c1 + n], ALU.mult)
+
+        first, second = [(0, 0), (1, 0)], [(0, 1), (1, 1)]
+        banks = [first_stage(0)]
+        put_y1(0, 0, 256)
+        keep_h1(0, banks[0], first)
+        banks.append(first_stage(1))
+        put_y1(1, 0, 256)
+        quantize_w3(1, nc.vector.tensor_copy)
+        keep_h1(0, banks[0], second)
+        put_y1(0, 256, 256)
+        put_y1(1, 256, 256)
+        banks.append(first_stage(2))
+        keep_h1(1, banks[1], first)
+        put_y1(2, 0, 512)
+        keep_h1(1, banks[1], second)
+        put_y1(3, 0, 512)
+        banks.append(first_stage(3))
+        keep_h1(2, banks[2], first)
+        put_y1(0, 512, 256)
+        keep_h1(2, banks[2], second)
+        put_y1(1, 512, 256)
+        keep_h1(3, banks[3], [(0, 0), (0, 1)])
+        put_y1(0, 768, 256)
+        keep_h1(3, banks[3], [(1, 0), (1, 1)])
+        put_y1(1, 768, 256)
+
+        z2_sum = {}
+        for b in range(2):
+            z2_sum[b] = wide([P, 4, PA], "z2_sum")
+            for t in range(4):
+                nc.vector.tensor_tensor(z2_sum[b][:, t, :], h1[b, t][:].indirect(p1[:]), gated[b][:, t, :], ALU.add)
+
+        z2_c, z2_sc = {}, {}
+        for b in range(2):
+            grouped = ring.tile([P, PA, 4], BF16, name="w_grouped", tag="w_grouped", bufs=2, align_bytes=64)
+            nc.scalar.copy(grouped[:].rearrange("p (c e) t -> p c t e", e=4), z2_sum[b][:].rearrange("p t (c e) -> p c t e", e=4))
+            z2_c[b] = keep([P, PA], U32, "z2_c%d" % b)
+            z2_sc[b] = keep([P, PA], U8, "z2_sc%d" % b)
+            quantize(z2_c[b][:], z2_sc[b][:], grouped[:].rearrange("p j t -> p (j t)"))
+            put_y1(2 + b, 512, 512, "h1_1%d" % (2 + b))
+
+        y2 = {}
+
+        def put_y2(nt):
+            nc.vector.tensor_tensor(page[nt][:].indirect(idx4[:]), y2[nt][:], wg2_sb[:], ALU.mult)
+            nc.sync.dma_start(out[P * nt : P * nt + P, :], page[nt][:])
+
+        for nt in range(4):
+            ya_bank = psum.tile([P, PA], F32, name="ya_bank", tag="bank0", bufs=3)
+            yb_bank = psum.tile([P, PA], F32, name="yb_bank", tag="bank1", bufs=3)
+            for b in range(2):
+                nc.tensor.matmul_mx(
+                    ya_bank[:],
+                    lhsT=w4_w[:, b, 2 * P * nt : 2 * P * nt + 2 * P].bitcast(FP4X4),
+                    lhsT_scale=w4_sc[:, N * b + P * nt : N * b + P * nt + P],
+                    rhs=z2_c[b][:].bitcast(FP8X4),
+                    rhs_scale=z2_sc[b][:],
+                    start=(b == 0),
+                    stop=(b == 1),
+                )
+            for b in range(2):
+                nc.tensor.matmul_mx(
+                    yb_bank[:],
+                    lhsT=w5_w[:, b, P * nt : P * nt + P].bitcast(FP8X4),
+                    lhsT_scale=w5_sc[:, N * b + P * nt : N * b + P * nt + P],
+                    rhs=z2_c[b][:].bitcast(FP8X4),
+                    rhs_scale=z2_sc[b][:],
+                    start=(b == 0),
+                    stop=(b == 1),
+                )
+            ya = ring.tile([P, PA], F32, name="y", tag="y", bufs=4, align_bytes=64)
+            nc.scalar.copy(ya[:], ya_bank[:])
+            y2[nt] = ring.tile([P, PA], F32, name="y2", tag="y2", bufs=3, align_bytes=64)
+            nc.vector.tensor_tensor(y2[nt][:], yb_bank[:], ya[:], ALU.mult)
+            if nt > 0:
+                put_y2(nt - 1)
+        put_y2(3)

@@ -113,7 +113,7 @@ def tile_list_wire_laundering_features_kernel(
 
         load_w1(0, 0)
         for q in range(4):
-            nc.sync.dma_start(tab_sc[32 * q : 32 * q + 8, :].bitcast(I32), tab_scales[:, 4 * q : 4 * q + 4, :].bitcast(I32))
+            nc.sync.dma_start(tab_sc[32 * q + 8 : 32 * q + 16, :].bitcast(I32), tab_scales[:, 4 * q : 4 * q + 4, :].bitcast(I32))
         amp_sb = keep([P, 2, 4], F32, "amp_sb")
         nc.sync.dma_start(amp_sb[:], amp.rearrange("(b p t) -> p b t", b=2, t=4))
         load_w1(1, 0)
@@ -124,8 +124,8 @@ def tile_list_wire_laundering_features_kernel(
         idx3 = load_list(offs3, "idx3")
         load_wg1(0)
         load_page(0)
-        load_page(1)
         load_w3(1)
+        load_page(1)
         load_page(2)
         load_page(3)
         load_wg1(1)
@@ -220,7 +220,7 @@ def tile_list_wire_laundering_features_kernel(
                                 lhsT=w1_c[a, b][:, P * t : P * t + P].bitcast(FP8X4),
                                 lhsT_scale=w1_sc[a, b][:, P * t : P * t + P],
                                 rhs=v_w[a][:, j0 : j0 + P].bitcast(FP8X4),
-                                rhs_scale=v_sc[4 * a : P, j0 : j0 + P],
+                                rhs_scale=v_sc[8 + 4 * a : P, j0 : j0 + P],
                                 start=(a == 1),
                                 stop=(a == 0),
                             )

@@ -121,10 +121,10 @@ def tile_list_wire_laundering_features_kernel(
         load_w1(1, 1)
         tab_w.append(load_words(tab_words[1], "tab_w1"))
         load_w3(0)
+        load_w3(1)
         idx3 = load_list(offs3, "idx3")
         load_wg1(0)
         load_page(0)
-        load_w3(1)
         load_page(1)
         load_page(2)
         load_page(3)
@@ -259,11 +259,11 @@ def tile_list_wire_laundering_features_kernel(
 
         first, second = [(0, 0), (1, 0)], [(0, 1), (1, 1)]
         banks = [first_stage(0)]
+        quantize_w3(1, nc.vector.tensor_copy)
         put_y1(0, 0, 256)
         keep_h1(0, banks[0], first)
         banks.append(first_stage(1))
         put_y1(1, 0, 256)
-        quantize_w3(1, nc.vector.tensor_copy)
         keep_h1(0, banks[0], second)
         put_y1(0, 256, 256)
         put_y1(1, 256, 256)

@@ -146,11 +146,11 @@ def tile_list_wire_laundering_features_kernel(
 
         def quantize_w1(a, b, split):
             grouped = ring.tile([P, 4, P, 4], BF16, name="w_grouped", tag="w_grouped", bufs=2, align_bytes=64)
-            dst = grouped[:].rearrange("p t m i -> p m t i")
-            src = w1_raw[a, b][:].rearrange("p i (m t) -> p m t i", t=4)
+            dst = grouped[:].rearrange("p (s e) m i -> p s m i e", e=2)
+            src = w1_raw[a, b][:].rearrange("p i (m s e) -> p s m i e", s=2, e=2)
             if split:
-                nc.scalar.copy(dst[:, :split], src[:, :split])
-            nc.vector.tensor_copy(dst[:, split:], src[:, split:])
+                nc.scalar.copy(dst[:, :, :split], src[:, :, :split])
+            nc.vector.tensor_copy(dst[:, :, split:], src[:, :, split:])
             w1_c[a, b] = keep([P, 512], U32, "w1_c%d%d" % (a, b))
             w1_sc[a, b] = keep([P, 512], U8, "w1_sc%d%d" % (a, b))
             quantize(w1_c[a, b][:], w1_sc[a, b][:], grouped[:].rearrange("p t m i -> p (t m i)"))

from contextlib import ExitStack

import concourse.mybir as mybir
from concourse.masks import make_identity

K, M, T, S, PA, H, N, T2 = 1024, 512, 2048, 1024, 512, 1024, 512, 2048
FLOPS = 2 * (K * H * S + M * H * PA + H * N * S + 2 * H * N * PA)

F32 = mybir.dt.float32
BF16 = mybir.dt.bfloat16
I32 = mybir.dt.int32
U32 = mybir.dt.uint32
U16 = mybir.dt.uint16
U8 = mybir.dt.uint8
FP8X4 = mybir.dt.float8_e4m3fn_x4
FP4X4 = mybir.dt.float4_e2m1fn_x4
ACT = mybir.ActivationFunctionType
ALU = mybir.AluOpType

P = 128


def tile_list_wire_laundering_features_kernel(
    tc, tab_words, tab_scales, tab2_words, tab2_scales, offs, offs2, pos1, offs3, offs4,
    w1, w2_words, w2_scales, amp, w3, w4_words, w4_scales, w5_words, w5_scales, page1, wg1, wg2, out,
):
    nc = tc.nc
    with ExitStack() as ctx:
        held = ctx.enter_context(tc.tile_pool(name="held", bufs=1))
        ring = ctx.enter_context(tc.tile_pool(name="ring", bufs=1))
        psum = ctx.enter_context(tc.psum_pool(name="psum", bufs=1))

        def keep(shape, dtype, name):
            return held.tile(shape, dtype, name=name, align_bytes=64)

        def wide(shape, name):
            return ring.tile(shape, F32, name=name, tag="wide", bufs=5, align_bytes=64)

        def load_list(src, name):
            lst = keep([P, src.shape[1]], U16, name)
            nc.sync.dma_start(lst[:], src)
            return lst

        def load_words(src, name):
            words = keep([P, src.shape[1]], I32, name)
            nc.sync.dma_start(words[:], src.rearrange("p t i -> p (t i)").bitcast(I32))
            return words

        def zeroed(width, name, engine):
            plane = keep([P, width], U8, name)
            engine.memset(plane[:].bitcast(I32), 0)
            return plane

        def load_scales_side_by_side(plane, src):
            passes = src.shape[0]
            for q in range(4):
                nc.sync.dma_start(
                    plane[32 * q : 32 * q + 4, :].bitcast(I32).rearrange("r (a c) -> r a c", a=passes),
                    src[:, 4 * q : 4 * q + 4, :].bitcast(I32).rearrange("a r c -> r a c"),
                )

        def gather_words(got, words, lst):
            nc.vector.tensor_copy(got, words[:].bitcast(U32).indirect(lst))

        def gather_scales(got, plane, lst):
            nc.vector.tensor_copy(got, plane[:].indirect(lst))

        def quantize(codes, scales, grouped):
            nc.vector.quantize_mx(out=codes.bitcast(FP8X4), scales=scales, in_=grouped)

        tab2_sc = zeroed(T, "tab2_sc", nc.gpsimd)
        w2_sc = zeroed(H, "w2_sc", nc.gpsimd)
        tab_sc = zeroed(T, "tab_sc", nc.vector)
        w4_sc = zeroed(2 * N, "w4_sc", nc.vector)
        w5_sc = zeroed(2 * N, "w5_sc", nc.vector)
        ident = keep([P, P], F32, "ident")
        make_identity(nc, ident[:])

        load_scales_side_by_side(tab2_sc, tab2_scales)
        idx2 = load_list(offs2, "idx2")
        tab2_w = load_words(tab2_words[0], "tab2_w")
        w2_w = keep([P, 2 * H], U8, "w2_w")
        nc.sync.dma_start(w2_w[:].bitcast(I32), w2_words[0].bitcast(I32))
        idx = load_list(offs, "idx")
        load_scales_side_by_side(w2_sc, w2_scales)
        tab_w = [load_words(tab_words[0], "tab_w0")]
        w1_raw = {}

        def load_w1(a, b):
            w1_raw[a, b] = wide([P, 4, 512], "w1_raw")
            rows = w1[512 * a : 512 * a + 512, 512 * b : 512 * b + 512]
            nc.sync.dma_start(w1_raw[a, b][:], rows.rearrange("(p i) c -> p i c", i=4))

        w3_raw = {}

        def load_w3(g):
            w3_raw[g] = wide([P, 2, 4, 256], "w3_raw")
            for b in range(2):
                rows = w3[512 * b : 512 * b + 512, 256 * g : 256 * g + 256]
                nc.sync.dma_start(w3_raw[g][:, b], rows.rearrange("(p i) c -> p i c", i=4))

        page = {}

        def load_page(nt):
            page[nt] = held.tile([P, T2], F32, name="page", tag="page%d" % nt, align_bytes=64)
            nc.sync.dma_start(page[nt][:], page1[P * nt : P * nt + P, :])

        wg1_sb = {}

        def load_wg1(h):
            wg1_sb[h] = keep([P, 512], F32, "wg1_sb%d" % h)
            nc.sync.dma_start(wg1_sb[h][:], wg1[:, 512 * h : 512 * h + 512])

        load_w1(0, 0)
        for q in range(4):
            nc.sync.dma_start(tab_sc[32 * q + 8 : 32 * q + 16, :].bitcast(I32), tab_scales[:, 4 * q : 4 * q + 4, :].bitcast(I32))
        amp_sb = keep([P, 2, 4], F32, "amp_sb")
        nc.sync.dma_start(amp_sb[:], amp.rearrange("(b p t) -> p b t", b=2, t=4))
        load_w1(1, 0)
        load_w1(0, 1)
        load_w1(1, 1)
        tab_w.append(load_words(tab_words[1], "tab_w1"))
        load_w3(0)
        load_w3(1)
        idx3 = load_list(offs3, "idx3")
        load_wg1(0)
        load_page(0)
        load_page(1)
        load_page(2)
        load_page(3)
        load_wg1(1)
        p1 = load_list(pos1, "p1")
        w4_w = keep([P, 2, 2 * N], U8, "w4_w")
        nc.sync.dma_start(w4_w[:].bitcast(I32), w4_words.bitcast(I32).rearrange("a p c -> p a c"))
        load_scales_side_by_side(w4_sc, w4_scales)
        w5_w = keep([P, 2, N], I32, "w5_w")
        nc.sync.dma_start(w5_w[:], w5_words.rearrange("a p c i -> p a (c i)").bitcast(I32))
        load_scales_side_by_side(w5_sc, w5_scales)
        wg2_sb = keep([P, PA], F32, "wg2_sb")
        nc.sync.dma_start(wg2_sb[:], wg2)
        idx4 = load_list(offs4, "idx4")

        w1_c, w1_sc = {}, {}
        v_w = [keep([P, S], U32, "v_w%d" % a) for a in range(2)]
        v_sc = keep([P, S], U8, "v_sc")

        def quantize_w1(a, b, split):
            grouped = ring.tile([P, 4, P, 4], BF16, name="w_grouped", tag="w_grouped", bufs=2, align_bytes=64)
            dst = grouped[:].rearrange("p (s e) m i -> p s m i e", e=2)
            src = w1_raw[a, b][:].rearrange("p i (m s e) -> p s m i e", s=2, e=2)
            if split:
                nc.scalar.copy(dst[:, :, :split], src[:, :, :split])
            nc.vector.tensor_copy(dst[:, :, split:], src[:, :, split:])
            w1_c[a, b] = keep([P, 512], U32, "w1_c%d%d" % (a, b))
            w1_sc[a, b] = keep([P, 512], U8, "w1_sc%d%d" % (a, b))
            quantize(w1_c[a, b][:], w1_sc[a, b][:], grouped[:].rearrange("p t m i -> p (t m i)"))

        w3_c, w3_sc = {}, {}

        def quantize_w3(g, copy):
            grouped = ring.tile([P, 2, 256, 4], BF16, name="w_grouped", tag="w_grouped", bufs=2, align_bytes=64)
            for b in range(2):
                copy(grouped[:, b].rearrange("p (c e) i -> p c i e", e=4), w3_raw[g][:, b].rearrange("p i (c e) -> p c i e", e=4))
            w3_c[g] = keep([P, 512], U32, "w3_c%d" % g)
            w3_sc[g] = keep([P, 512], U8, "w3_sc%d" % g)
            quantize(w3_c[g][:], w3_sc[g][:], grouped[:].rearrange("p b c i -> p (b c i)"))

        v2_w = keep([P, PA], U32, "v2_w")
        v2_sc = keep([P, PA], U8, "v2_sc")
        gather_words(v2_w[:], tab2_w, idx2[:])
        gather_scales(v2_sc[:], tab2_sc, idx2[:])
        tanh_t, gated = {}, {}
        for b in range(2):
            for u in range(4):
                tanh_t[b, u] = ring.tile([P, 4, P], F32, name="tanh_t", tag=("y", "z1_grouped")[b], bufs=4, align_bytes=64)
                bank = psum.tile([P, 512], F32, name="h2_bank", tag="bank0", bufs=3)
                nc.tensor.matmul_mx(
                    bank[:],
                    lhsT=v2_w[:, P * u : P * u + P].bitcast(FP8X4),
                    lhsT_scale=v2_sc[:, P * u : P * u + P],
                    rhs=w2_w[:, 1024 * b : 1024 * b + 1024].bitcast(FP4X4),
                    rhs_scale=w2_sc[:, 512 * b : 512 * b + 512],
                    start=True,
                    stop=True,
                )
                nc.scalar.activation(tanh_t[b, u][:], bank[:].rearrange("p (m t) -> p t m", t=4), ACT.Tanh)
        for b in range(2):
            gated[b] = keep([P, 4, PA], F32, "gated%d" % b)
            for t in range(4):
                bank = psum.tile([P, 512], F32, name="turn_bank", tag="bank1", bufs=3)
                for u in range(4):
                    nc.tensor.transpose(bank[:, P * u : P * u + P], tanh_t[b, u][:, t, :], ident[:])
                nc.scalar.activation(gated[b][:, t, :], bank[:], ACT.Copy, scale=amp_sb[:, b, t : t + 1])

        gather_words(v_w[0][:], tab_w[0], idx[:])
        gather_scales(v_sc[:], tab_sc, idx[:])
        quantize_w1(0, 0, 0)
        quantize_w1(1, 0, 0)
        quantize_w1(0, 1, 0)
        quantize_w1(1, 1, 96)
        for j0, n in ((0, 256), (256, 256), (512, 512)):
            gather_words(v_w[1][:, j0 : j0 + n], tab_w[1], idx[:, j0 // 16 : (j0 + n) // 16])
        quantize_w3(0, nc.vector.tensor_copy)

        h1 = {(b, t): held.tile([P, S], F32, name="h1", tag="h1_%d%d" % (b, t), align_bytes=64) for b in range(2) for t in range(4)}
        z1_c = [keep([P, S], U32, "z1_c%d" % b) for b in range(2)]
        z1_sc = [keep([P, S], U8, "z1_sc%d" % b) for b in range(2)]

        def first_stage(jq):
            banks = {}
            for b in range(2):
                grouped = ring.tile([P, 256, 4], BF16, name="z1_grouped", tag="z1_grouped", bufs=4, align_bytes=64)
                for u in range(2):
                    j0 = 256 * jq + P * u
                    bank = psum.tile([P, 4, P], F32, name="h1_bank", tag="bank%d" % b, bufs=3)
                    for t in range(4):
                        for a in (1, 0):
                            nc.tensor.matmul_mx(
                                bank[:, t, :],
                                lhsT=w1_c[a, b][:, P * t : P * t + P].bitcast(FP8X4),
                                lhsT_scale=w1_sc[a, b][:, P * t : P * t + P],
                                rhs=v_w[a][:, j0 : j0 + P].bitcast(FP8X4),
                                rhs_scale=v_sc[8 + 4 * a : P, j0 : j0 + P],
                                start=(a == 1),
                                stop=(a == 0),
                            )
                    nc.scalar.activation(grouped[:, P * u : P * u + P, :], bank[:].rearrange("p t j -> p j t"), ACT.Abs)
                    banks[b, u] = bank
                cols = slice(256 * jq, 256 * jq + 256)
                quantize(z1_c[b][:, cols], z1_sc[b][:, cols], grouped[:].rearrange("p j t -> p (j t)"))
            return banks

        def keep_h1(jq, banks, which):
            for b, u in which:
                j0 = 256 * jq + P * u
                for t in range(4):
                    nc.scalar.copy(h1[b, t][:, j0 : j0 + P], banks[b, u][:, t, :])

        def put_y1(nt, j0, n, behind=None):
            g, c0 = divmod(P * nt, 256)
            bank = psum.tile([P, 512], F32, name="y_bank", tag="y_bank", bufs=2)
            for b in range(2):
                nc.tensor.matmul_mx(
                    bank[:, 0:n],
                    lhsT=w3_c[g][:, 256 * b + c0 : 256 * b + c0 + P].bitcast(FP8X4),
                    lhsT_scale=w3_sc[g][:, 256 * b + c0 : 256 * b + c0 + P],
                    rhs=z1_c[b][:, j0 : j0 + n].bitcast(FP8X4),
                    rhs_scale=z1_sc[b][:, j0 : j0 + n],
                    start=(b == 0),
                    stop=(b == 1),
                )
            if behind is None:
                y = ring.tile([P, n], F32, name="y", tag="y", bufs=4, align_bytes=64)
            else:
                y = held.tile([P, n], F32, name="y", tag=behind, align_bytes=64)
            nc.scalar.copy(y[:], bank[:, 0:n])
            h, c1 = divmod(j0, 512)
            nc.vector.tensor_tensor(page[nt][:].indirect(idx3[:, j0 // 16 : (j0 + n) // 16]), y[:], wg1_sb[h][:, c1 : c1 + n], ALU.mult)

        first, second = [(0, 0), (1, 0)], [(0, 1), (1, 1)]
        banks = [first_stage(0)]
        quantize_w3(1, nc.vector.tensor_copy)
        put_y1(0, 0, 256)
        keep_h1(0, banks[0], first)
        banks.append(first_stage(1))
        put_y1(1, 0, 256)
        keep_h1(0, banks[0], second)
        put_y1(0, 256, 256)
        put_y1(1, 256, 256)
        banks.append(first_stage(2))
        keep_h1(1, banks[1], first)
        put_y1(2, 0, 512)
        keep_h1(1, banks[1], second)
        put_y1(3, 0, 512)
        banks.append(first_stage(3))
        keep_h1(2, banks[2], first)
        put_y1(0, 512, 256)
        keep_h1(2, banks[2], second)
        put_y1(1, 512, 256)
        keep_h1(3, banks[3], [(0, 0), (0, 1)])
        put_y1(0, 768, 256)
        keep_h1(3, banks[3], [(1, 0), (1, 1)])
        put_y1(1, 768, 256)

        z2_sum = {}
        for b in range(2):
            z2_sum[b] = wide([P, 4, PA], "z2_sum")
            for t in range(4):
                nc.vector.tensor_tensor(z2_sum[b][:, t, :], h1[b, t][:].indirect(p1[:]), gated[b][:, t, :], ALU.add)

        z2_c, z2_sc = {}, {}
        for b in range(2):
            grouped = ring.tile([P, PA, 4], BF16, name="w_grouped", tag="w_grouped", bufs=2, align_bytes=64)
            nc.scalar.copy(grouped[:].rearrange("p (c e) t -> p c t e", e=4), z2_sum[b][:].rearrange("p t (c e) -> p c t e", e=4))
            z2_c[b] = keep([P, PA], U32, "z2_c%d" % b)
            z2_sc[b] = keep([P, PA], U8, "z2_sc%d" % b)
            quantize(z2_c[b][:], z2_sc[b][:], grouped[:].rearrange("p j t -> p (j t)"))
            put_y1(2 + b, 512, 512, "h1_1%d" % (2 + b))

        y2 = {}

        def put_y2(nt):
            nc.vector.tensor_tensor(page[nt][:].indirect(idx4[:]), y2[nt][:], wg2_sb[:], ALU.mult)
            nc.sync.dma_start(out[P * nt : P * nt + P, :], page[nt][:])

        for nt in range(4):
            ya_bank = psum.tile([P, PA], F32, name="ya_bank", tag="bank0", bufs=3)
            yb_bank = psum.tile([P, PA], F32, name="yb_bank", tag="bank1", bufs=3)
            for b in range(2):
                nc.tensor.matmul_mx(
                    ya_bank[:],
                    lhsT=w4_w[:, b, 2 * P * nt : 2 * P * nt + 2 * P].bitcast(FP4X4),
                    lhsT_scale=w4_sc[:, N * b + P * nt : N * b + P * nt + P],
                    rhs=z2_c[b][:].bitcast(FP8X4),
                    rhs_scale=z2_sc[b][:],
                    start=(b == 0),
                    stop=(b == 1),
                )
            for b in range(2):
                nc.tensor.matmul_mx(
                    yb_bank[:],
                    lhsT=w5_w[:, b, P * nt : P * nt + P].bitcast(FP8X4),
                    lhsT_scale=w5_sc[:, N * b + P * nt : N * b + P * nt + P],
                    rhs=z2_c[b][:].bitcast(FP8X4),
                    rhs_scale=z2_sc[b][:],
                    start=(b == 0),
                    stop=(b == 1),
                )
            ya = ring.tile([P, PA], F32, name="y", tag="y", bufs=4, align_bytes=64)
            nc.scalar.copy(ya[:], ya_bank[:])
            y2[nt] = ring.tile([P, PA], F32, name="y2", tag="y2", bufs=3, align_bytes=64)
            nc.vector.tensor_tensor(y2[nt][:], yb_bank[:], ya[:], ALU.mult)
            if nt > 0:
                put_y2(nt - 1)
        put_y2(3)
